import numpy as np
import ml_dtypes


def mxq(x, axis, fmt="e4m3"):
    dtype, down = {"e4m3": (ml_dtypes.float8_e4m3fn, 7), "e5m2": (ml_dtypes.float8_e5m2, 14)}[fmt]
    v = np.moveaxis(np.asarray(x, np.float32).astype(ml_dtypes.bfloat16).astype(np.float64), axis, -1)
    blocks = v.reshape(v.shape[:-1] + (-1, 32))
    amax = np.abs(blocks).max(-1, keepdims=True)
    byte = np.maximum(np.where(amax > 0, np.frexp(amax)[1] - 1 + 127, 0) - down, 1)
    scale = np.exp2(byte - 127.0)
    codes = (blocks / scale).astype(np.float32).astype(dtype).astype(np.float64)
    return np.moveaxis((codes * scale).reshape(v.shape), -1, axis)


WIDE = False


def mx_kscale(k):
    if not WIDE:
        return np.ones(k)
    levels = np.array([10, -10, 5, -5, 0])
    if k % 512:
        return np.exp2(np.random.permutation(np.resize(levels, k // 32))).repeat(32)
    a = np.empty((k // 512, 16))
    for p in range(k // 512):
        a[p, :8] = np.random.permutation(np.resize(levels, 8))
        for g in range(8):
            far = levels[np.abs(levels - a[p, g]) >= 10]
            a[p, g + 8] = far[np.random.randint(len(far))]
    return np.exp2(a.ravel()).repeat(32)


def f64(x):
    return np.asarray(x).astype(np.float64)


def striped(idx):
    return np.tile(idx.reshape(-1, 16).T, (8, 1)).astype(np.uint16)


def unstriped(offs):
    return offs[:16].T.reshape(-1).astype(np.int64)


def gelu(v):
    return 0.5 * v * (1.0 + np.tanh(np.sqrt(2.0 / np.pi) * (v + 0.044715 * v**3)))


K, T, S, N = 512, 256, 512, 2048


def setup_inputs():
    n = np.random.standard_normal
    s = mx_kscale(K)[:, None]
    return {
        "w": (n((K, N)) / np.sqrt(K) / s).astype(np.float32),
        "xT": (n((K, T)) * s).astype(np.float32),
        "b": (0.3 * n((S, 1))).astype(np.float32),
        "offs": striped(np.sort(np.random.permutation(N)[:S])),
    }


def reference(w, xT, b, offs):
    idx = unstriped(offs)
    wq = mxq(f64(w)[:, idx], 0, "e4m3")
    return gelu((wq.T @ mxq(f64(xT), 0, "e4m3")) + f64(b))

@@ -1,0 +1,105 @@
+from contextlib import ExitStack
+
+import concourse.mybir as mybir
+from concourse.masks import make_identity
+
+K, N, S, T = 512, 2048, 512, 256
+FLOPS = 2 * K * S * T
+
+F32 = mybir.dt.float32
+BF16 = mybir.dt.bfloat16
+U32 = mybir.dt.uint32
+U16 = mybir.dt.uint16
+U8 = mybir.dt.uint8
+FP8X4 = mybir.dt.float8_e4m3fn_x4
+ACT = mybir.ActivationFunctionType
+
+P = 128
+PACK = 4
+HALF = S // 2
+M_TILES = S // P
+
+
+def tile_picked_neuron_lin_gelu_srt_e_kernel(tc, w, xT, b, offs, out):
+    nc = tc.nc
+    with ExitStack() as ctx:
+        keep = ctx.enter_context(tc.tile_pool(name="keep", bufs=1))
+        psum = ctx.enter_context(tc.psum_pool(name="psum", bufs=1))
+
+        offsets = keep.tile([P, S // 16], U16, name="offsets")
+        nc.sync.dma_start(offsets[:], offs)
+        w_rows = w.rearrange("(p j) n -> p j n", j=PACK)
+        planes = []
+        for j in range(PACK):
+            plane = keep.tile([P, N], F32, name=f"plane{j}", align_bytes=64)
+            nc.sync.dma_start(out=plane[:], in_=w_rows[:, j, :])
+            planes.append(plane)
+        x_raw = keep.tile([P, PACK, T], F32, name="x_raw", align_bytes=64)
+        nc.sync.dma_start(out=x_raw[:], in_=xT.rearrange("(p j) t -> p j t", j=PACK))
+
+        b_rows = keep.tile([P, P], F32, name="b_rows", align_bytes=64)
+        nc.vector.memset(b_rows[:], 0.0)
+        warm = keep.tile([P, 1], F32, name="warm")
+        nc.vector.memset(warm[:], 0.0)
+        nc.scalar.dma_start(out=b_rows[0:M_TILES, :], in_=b.rearrange("(m p) o -> m (p o)", p=P))
+        ident = keep.tile([P, P], F32, name="ident", align_bytes=64)
+        make_identity(nc, ident[:])
+        table = keep.tile([P, 1], F32, name="table")
+        nc.scalar.activation(out=table[:], in_=warm[:], func=ACT.Gelu_apprx_tanh)
+        b_turned = psum.tile([P, P], F32, name="b_turned", tag="bank3_128")
+        nc.tensor.transpose(b_turned[:], b_rows[:], ident[:])
+        bias = keep.tile([P, M_TILES], F32, name="bias")
+        nc.scalar.copy(out=bias[:], in_=b_turned[:, 0:M_TILES])
+
+        w_bf = keep.tile([P, S, PACK], BF16, name="w_bf", align_bytes=64)
+        for j in range(PACK - 1):
+            nc.vector.tensor_copy(out=w_bf[:, :, j], in_=planes[j][:].indirect(offsets[:]))
+        for h in range(2):
+            nc.vector.tensor_copy(
+                out=w_bf[:, h * HALF : (h + 1) * HALF, PACK - 1],
+                in_=planes[PACK - 1][:].indirect(offsets[:, h * HALF // 16 : (h + 1) * HALF // 16]),
+            )
+
+        x_bf = keep.tile([P, T, PACK], BF16, name="x_bf", align_bytes=64)
+        for t0 in range(0, T, P):
+            nc.scalar.copy(out=x_bf[:, t0 : t0 + P, :], in_=x_raw[:, :, t0 : t0 + P].rearrange("p j t -> p t j"))
+
+        w_codes = keep.tile([P, S], U32, name="w_codes", align_bytes=64)
+        w_scales = keep.tile([P, S], U8, name="w_scales", align_bytes=64)
+        x_codes = keep.tile([P, T], U32, name="x_codes", align_bytes=64)
+        x_scales = keep.tile([P, T], U8, name="x_scales", align_bytes=64)
+
+        def quantise(codes, scales, values, c0):
+            cols = slice(c0, c0 + P)
+            nc.vector.quantize_mx(
+                out=codes[:, cols].bitcast(FP8X4),
+                scales=scales[:, cols],
+                in_=values[:, cols, :].rearrange("p c j -> p (c j)"),
+            )
+
+        quantise(w_codes, w_scales, w_bf, 0)
+        quantise(x_codes, x_scales, x_bf, 0)
+        for c0 in range(P, S, P):
+            quantise(w_codes, w_scales, w_bf, c0)
+        quantise(x_codes, x_scales, x_bf, P)
+
+        results = [keep.tile([P, T], F32, name=f"result{m}", align_bytes=64) for m in range(M_TILES)]
+        for t0 in range(0, T, P):
+            tokens = slice(t0, t0 + P)
+            for m in range(M_TILES):
+                cols = slice(m * P, (m + 1) * P)
+                acc = psum.tile([P, P], F32, name=f"acc{m}_{t0}", tag=f"bank{m}_{t0}")
+                nc.tensor.matmul_mx(
+                    out=acc[:],
+                    lhsT=w_codes[:, cols].bitcast(FP8X4),
+                    lhsT_scale=w_scales[:, cols],
+                    rhs=x_codes[:, tokens].bitcast(FP8X4),
+                    rhs_scale=x_scales[:, tokens],
+                    start=True,
+                    stop=True,
+                )
+                nc.scalar.activation(
+                    out=results[m][:, tokens], in_=acc[:], func=ACT.Gelu_apprx_tanh, bias=bias[:, m : m + 1]
+                )
+                if t0 + P == T:
+                    nc.sync.dma_start(out=out[cols, :], in_=results[m][:])

@@ -18,6 +18,7 @@ P = 128
 PACK = 4
 HALF = S // 2
 M_TILES = S // P
+PREFIX = N - HALF
 
 
 def tile_picked_neuron_lin_gelu_srt_e_kernel(tc, w, xT, b, offs, out):
@@ -26,16 +27,22 @@ def tile_picked_neuron_lin_gelu_srt_e_kernel(tc, w, xT, b, offs, out):
         keep = ctx.enter_context(tc.tile_pool(name="keep", bufs=1))
         psum = ctx.enter_context(tc.psum_pool(name="psum", bufs=1))
 
-        offsets = keep.tile([P, S // 16], U16, name="offsets")
-        nc.sync.dma_start(offsets[:], offs)
         w_rows = w.rearrange("(p j) n -> p j n", j=PACK)
-        planes = []
-        for j in range(PACK):
-            plane = keep.tile([P, N], F32, name=f"plane{j}", align_bytes=64)
-            nc.sync.dma_start(out=plane[:], in_=w_rows[:, j, :])
-            planes.append(plane)
-        x_raw = keep.tile([P, PACK, T], F32, name="x_raw", align_bytes=64)
-        nc.sync.dma_start(out=x_raw[:], in_=xT.rearrange("(p j) t -> p j t", j=PACK))
+        x_rows = xT.rearrange("(p j) t -> p j t", j=PACK)
+        planes = [keep.tile([P, N], F32, name=f"plane{j}", align_bytes=64) for j in range(PACK)]
+        offsets = keep.tile([P, S // 16], U16, name="offsets")
+        nc.sync.dma_start(out=planes[0][:], in_=w_rows[:, 0, :])
+        nc.sync.dma_start(offsets[:], offs)
+        for j in range(1, PACK - 1):
+            nc.sync.dma_start(out=planes[j][:], in_=w_rows[:, j, :])
+        last = planes[PACK - 1]
+        nc.sync.dma_start(out=last[:, :PREFIX], in_=w_rows[:, PACK - 1, :PREFIX])
+        nc.sync.dma_start(out=last[:, PREFIX:], in_=w_rows[:, PACK - 1, PREFIX:])
+        x_raw = []
+        for h in range(2):
+            raw = keep.tile([P, PACK, P], F32, name=f"x_raw{h}", tag=f"x_raw{h}", align_bytes=64)
+            nc.sync.dma_start(out=raw[:], in_=x_rows[:, :, h * P : (h + 1) * P])
+            x_raw.append(raw)
 
         b_rows = keep.tile([P, P], F32, name="b_rows", align_bytes=64)
         nc.vector.memset(b_rows[:], 0.0)
@@ -46,7 +53,7 @@ def tile_picked_neuron_lin_gelu_srt_e_kernel(tc, w, xT, b, offs, out):
         make_identity(nc, ident[:])
         table = keep.tile([P, 1], F32, name="table")
         nc.scalar.activation(out=table[:], in_=warm[:], func=ACT.Gelu_apprx_tanh)
-        b_turned = psum.tile([P, P], F32, name="b_turned", tag="bank3_128")
+        b_turned = psum.tile([P, P], F32, name="b_turned", tag="bank3_1")
         nc.tensor.transpose(b_turned[:], b_rows[:], ident[:])
         bias = keep.tile([P, M_TILES], F32, name="bias")
         nc.scalar.copy(out=bias[:], in_=b_turned[:, 0:M_TILES])
@@ -54,52 +61,64 @@ def tile_picked_neuron_lin_gelu_srt_e_kernel(tc, w, xT, b, offs, out):
         w_bf = keep.tile([P, S, PACK], BF16, name="w_bf", align_bytes=64)
         for j in range(PACK - 1):
             nc.vector.tensor_copy(out=w_bf[:, :, j], in_=planes[j][:].indirect(offsets[:]))
-        for h in range(2):
-            nc.vector.tensor_copy(
-                out=w_bf[:, h * HALF : (h + 1) * HALF, PACK - 1],
-                in_=planes[PACK - 1][:].indirect(offsets[:, h * HALF // 16 : (h + 1) * HALF // 16]),
-            )
+        nc.vector.tensor_copy(out=w_bf[:, :HALF, PACK - 1], in_=last[:, :PREFIX].indirect(offsets[:, : HALF // 16]))
+        nc.vector.tensor_copy(out=w_bf[:, HALF:, PACK - 1], in_=last[:].indirect(offsets[:, HALF // 16 :]))
 
         x_bf = keep.tile([P, T, PACK], BF16, name="x_bf", align_bytes=64)
-        for t0 in range(0, T, P):
-            nc.scalar.copy(out=x_bf[:, t0 : t0 + P, :], in_=x_raw[:, :, t0 : t0 + P].rearrange("p j t -> p t j"))
+        for h in range(2):
+            nc.scalar.copy(out=x_bf[:, h * P : (h + 1) * P, :], in_=x_raw[h][:].rearrange("p j t -> p t j"))
 
-        w_codes = keep.tile([P, S], U32, name="w_codes", align_bytes=64)
+        early = keep.tile([P, (M_TILES - 1) * P], U32, name="w_codes_early", tag="x_raw0", align_bytes=64)
+        late = keep.tile([P, P], U32, name="w_codes_late", tag="x_raw1", align_bytes=64)
+        w_codes = [early[:, m * P : (m + 1) * P] for m in range(M_TILES - 1)] + [late[:]]
         w_scales = keep.tile([P, S], U8, name="w_scales", align_bytes=64)
         x_codes = keep.tile([P, T], U32, name="x_codes", align_bytes=64)
         x_scales = keep.tile([P, T], U8, name="x_scales", align_bytes=64)
 
-        def quantise(codes, scales, values, c0):
-            cols = slice(c0, c0 + P)
+        def quantise(codes, scales, values, i):
+            cols = slice(i * P, (i + 1) * P)
             nc.vector.quantize_mx(
-                out=codes[:, cols].bitcast(FP8X4),
+                out=codes.bitcast(FP8X4),
                 scales=scales[:, cols],
                 in_=values[:, cols, :].rearrange("p c j -> p (c j)"),
             )
 
-        quantise(w_codes, w_scales, w_bf, 0)
-        quantise(x_codes, x_scales, x_bf, 0)
-        for c0 in range(P, S, P):
-            quantise(w_codes, w_scales, w_bf, c0)
-        quantise(x_codes, x_scales, x_bf, P)
+        def quantise_w(m):
+            quantise(w_codes[m], w_scales, w_bf, m)
+
+        def quantise_x(h):
+            quantise(x_codes[:, h * P : (h + 1) * P], x_scales, x_bf, h)
+
+        quantise_w(0)
+        quantise_x(0)
+        for m in range(1, M_TILES - 1):
+            quantise_w(m)
+        quantise_x(1)
+        quantise_w(M_TILES - 1)
 
         results = [keep.tile([P, T], F32, name=f"result{m}", align_bytes=64) for m in range(M_TILES)]
-        for t0 in range(0, T, P):
-            tokens = slice(t0, t0 + P)
-            for m in range(M_TILES):
-                cols = slice(m * P, (m + 1) * P)
-                acc = psum.tile([P, P], F32, name=f"acc{m}_{t0}", tag=f"bank{m}_{t0}")
-                nc.tensor.matmul_mx(
-                    out=acc[:],
-                    lhsT=w_codes[:, cols].bitcast(FP8X4),
-                    lhsT_scale=w_scales[:, cols],
-                    rhs=x_codes[:, tokens].bitcast(FP8X4),
-                    rhs_scale=x_scales[:, tokens],
-                    start=True,
-                    stop=True,
-                )
-                nc.scalar.activation(
-                    out=results[m][:, tokens], in_=acc[:], func=ACT.Gelu_apprx_tanh, bias=bias[:, m : m + 1]
-                )
-                if t0 + P == T:
-                    nc.sync.dma_start(out=out[cols, :], in_=results[m][:])
+
+        def product(m, h):
+            tokens = slice(h * P, (h + 1) * P)
+            cols = slice(m * P, (m + 1) * P)
+            acc = psum.tile([P, P], F32, name=f"acc{m}_{h}", tag=f"bank{m}_{h}")
+            nc.tensor.matmul_mx(
+                out=acc[:],
+                lhsT=w_codes[m].bitcast(FP8X4),
+                lhsT_scale=w_scales[:, cols],
+                rhs=x_codes[:, tokens].bitcast(FP8X4),
+                rhs_scale=x_scales[:, tokens],
+                start=True,
+                stop=True,
+            )
+            nc.scalar.activation(
+                out=results[m][:, tokens], in_=acc[:], func=ACT.Gelu_apprx_tanh, bias=bias[:, m : m + 1]
+            )
+            if h == 1:
+                nc.sync.dma_start(out=out[cols, :], in_=results[m][:])
+
+        for h in range(2):
+            for m in range(M_TILES - 1):
+                product(m, h)
+        for h in range(2):
+            product(M_TILES - 1, h)

@@ -37,9 +37,10 @@ def tile_picked_neuron_lin_gelu_srt_e_kernel(tc, w, xT, b, offs, out):
             nc.sync.dma_start(out=planes[j][:], in_=w_rows[:, j, :])
         last = planes[PACK - 1]
         nc.sync.dma_start(out=last[:, :PREFIX], in_=w_rows[:, PACK - 1, :PREFIX])
-        nc.sync.dma_start(out=last[:, PREFIX:], in_=w_rows[:, PACK - 1, PREFIX:])
         x_raw = []
         for h in range(2):
+            if h == 1:
+                nc.sync.dma_start(out=last[:, PREFIX:], in_=w_rows[:, PACK - 1, PREFIX:])
             raw = keep.tile([P, PACK, P], F32, name=f"x_raw{h}", tag=f"x_raw{h}", align_bytes=64)
             nc.sync.dma_start(out=raw[:], in_=x_rows[:, :, h * P : (h + 1) * P])
             x_raw.append(raw)
@@ -53,7 +54,7 @@ def tile_picked_neuron_lin_gelu_srt_e_kernel(tc, w, xT, b, offs, out):
         make_identity(nc, ident[:])
         table = keep.tile([P, 1], F32, name="table")
         nc.scalar.activation(out=table[:], in_=warm[:], func=ACT.Gelu_apprx_tanh)
-        b_turned = psum.tile([P, P], F32, name="b_turned", tag="bank3_1")
+        b_turned = psum.tile([P, P], F32, name="b_turned", tag="bias_bank")
         nc.tensor.transpose(b_turned[:], b_rows[:], ident[:])
         bias = keep.tile([P, M_TILES], F32, name="bias")
         nc.scalar.copy(out=bias[:], in_=b_turned[:, 0:M_TILES])
@@ -68,9 +69,8 @@ def tile_picked_neuron_lin_gelu_srt_e_kernel(tc, w, xT, b, offs, out):
         for h in range(2):
             nc.scalar.copy(out=x_bf[:, h * P : (h + 1) * P, :], in_=x_raw[h][:].rearrange("p j t -> p t j"))
 
-        early = keep.tile([P, (M_TILES - 1) * P], U32, name="w_codes_early", tag="x_raw0", align_bytes=64)
-        late = keep.tile([P, P], U32, name="w_codes_late", tag="x_raw1", align_bytes=64)
-        w_codes = [early[:, m * P : (m + 1) * P] for m in range(M_TILES - 1)] + [late[:]]
+        halves = [keep.tile([P, HALF], U32, name=f"w_codes{h}", tag=f"x_raw{h}", align_bytes=64) for h in range(2)]
+        w_codes = [halves[m // 2][:, (m % 2) * P : (m % 2 + 1) * P] for m in range(M_TILES)]
         w_scales = keep.tile([P, S], U8, name="w_scales", align_bytes=64)
         x_codes = keep.tile([P, T], U32, name="x_codes", align_bytes=64)
         x_scales = keep.tile([P, T], U8, name="x_scales", align_bytes=64)
@@ -91,17 +91,19 @@ def tile_picked_neuron_lin_gelu_srt_e_kernel(tc, w, xT, b, offs, out):
 
         quantise_w(0)
         quantise_x(0)
-        for m in range(1, M_TILES - 1):
-            quantise_w(m)
+        quantise_w(1)
         quantise_x(1)
-        quantise_w(M_TILES - 1)
+        quantise_w(2)
+        quantise_w(3)
 
-        results = [keep.tile([P, T], F32, name=f"result{m}", align_bytes=64) for m in range(M_TILES)]
+        firsts = [keep.tile([P, 2, P], F32, name=f"first{h}", align_bytes=64) for h in range(2)]
+        results = [keep.tile([P, T], F32, name=f"result{m}", align_bytes=64) for m in range(2)]
+        out_tiles = out.rearrange("(m p) t -> p m t", p=P)
 
-        def product(m, h):
-            tokens = slice(h * P, (h + 1) * P)
+        def product(m, t0, t1, result):
+            tokens = slice(t0, t1)
             cols = slice(m * P, (m + 1) * P)
-            acc = psum.tile([P, P], F32, name=f"acc{m}_{h}", tag=f"bank{m}_{h}")
+            acc = psum.tile([P, t1 - t0], F32, name=f"acc{m}_{t0}", tag=f"bank{m}_{t0}")
             nc.tensor.matmul_mx(
                 out=acc[:],
                 lhsT=w_codes[m].bitcast(FP8X4),
@@ -112,13 +114,15 @@ def tile_picked_neuron_lin_gelu_srt_e_kernel(tc, w, xT, b, offs, out):
                 stop=True,
             )
             nc.scalar.activation(
-                out=results[m][:, tokens], in_=acc[:], func=ACT.Gelu_apprx_tanh, bias=bias[:, m : m + 1]
+                out=result, in_=acc[:], func=ACT.Gelu_apprx_tanh, bias=bias[:, m : m + 1]
             )
-            if h == 1:
-                nc.sync.dma_start(out=out[cols, :], in_=results[m][:])
 
         for h in range(2):
-            for m in range(M_TILES - 1):
-                product(m, h)
-        for h in range(2):
-            product(M_TILES - 1, h)
+            for m in range(2):
+                product(m, h * P, (h + 1) * P, firsts[h][:, m, :])
+            nc.sync.dma_start(out=out_tiles[:, 0:2, h * P : (h + 1) * P], in_=firsts[h][:])
+        product(2, 0, T, results[0][:])
+        nc.sync.dma_start(out=out_tiles[:, 2, :], in_=results[0][:])
+        for t0 in range(0, T, P):
+            product(3, t0, t0 + P, results[1][:, t0 : t0 + P])
+        nc.sync.dma_start(out=out_tiles[:, 3, :], in_=results[1][:])

@@ -54,7 +54,7 @@ def tile_picked_neuron_lin_gelu_srt_e_kernel(tc, w, xT, b, offs, out):
         make_identity(nc, ident[:])
         table = keep.tile([P, 1], F32, name="table")
         nc.scalar.activation(out=table[:], in_=warm[:], func=ACT.Gelu_apprx_tanh)
-        b_turned = psum.tile([P, P], F32, name="b_turned", tag="bias_bank")
+        b_turned = psum.tile([P, P], F32, name="b_turned", tag="bank3_128")
         nc.tensor.transpose(b_turned[:], b_rows[:], ident[:])
         bias = keep.tile([P, M_TILES], F32, name="bias")
         nc.scalar.copy(out=bias[:], in_=b_turned[:, 0:M_TILES])
@@ -69,8 +69,8 @@ def tile_picked_neuron_lin_gelu_srt_e_kernel(tc, w, xT, b, offs, out):
         for h in range(2):
             nc.scalar.copy(out=x_bf[:, h * P : (h + 1) * P, :], in_=x_raw[h][:].rearrange("p j t -> p t j"))
 
-        halves = [keep.tile([P, HALF], U32, name=f"w_codes{h}", tag=f"x_raw{h}", align_bytes=64) for h in range(2)]
-        w_codes = [halves[m // 2][:, (m % 2) * P : (m % 2 + 1) * P] for m in range(M_TILES)]
+        codes = keep.tile([P, S], U32, name="w_codes", tag="x_raw0", align_bytes=64)
+        w_codes = [codes[:, m * P : (m + 1) * P] for m in range(M_TILES)]
         w_scales = keep.tile([P, S], U8, name="w_scales", align_bytes=64)
         x_codes = keep.tile([P, T], U32, name="x_codes", align_bytes=64)
         x_scales = keep.tile([P, T], U8, name="x_scales", align_bytes=64)
@@ -91,13 +91,10 @@ def tile_picked_neuron_lin_gelu_srt_e_kernel(tc, w, xT, b, offs, out):
 
         quantise_w(0)
         quantise_x(0)
-        quantise_w(1)
+        for m in range(1, M_TILES):
+            quantise_w(m)
         quantise_x(1)
-        quantise_w(2)
-        quantise_w(3)
 
-        firsts = [keep.tile([P, 2, P], F32, name=f"first{h}", align_bytes=64) for h in range(2)]
-        results = [keep.tile([P, T], F32, name=f"result{m}", align_bytes=64) for m in range(2)]
         out_tiles = out.rearrange("(m p) t -> p m t", p=P)
 
         def product(m, t0, t1, result):
@@ -117,12 +114,9 @@ def tile_picked_neuron_lin_gelu_srt_e_kernel(tc, w, xT, b, offs, out):
                 out=result, in_=acc[:], func=ACT.Gelu_apprx_tanh, bias=bias[:, m : m + 1]
             )
 
-        for h in range(2):
-            for m in range(2):
-                product(m, h * P, (h + 1) * P, firsts[h][:, m, :])
-            nc.sync.dma_start(out=out_tiles[:, 0:2, h * P : (h + 1) * P], in_=firsts[h][:])
-        product(2, 0, T, results[0][:])
-        nc.sync.dma_start(out=out_tiles[:, 2, :], in_=results[0][:])
         for t0 in range(0, T, P):
-            product(3, t0, t0 + P, results[1][:, t0 : t0 + P])
-        nc.sync.dma_start(out=out_tiles[:, 3, :], in_=results[1][:])
+            for m0 in range(0, M_TILES, 2):
+                result = keep.tile([P, 2, P], F32, name=f"result{m0}_{t0}", align_bytes=64)
+                for i in range(2):
+                    product(m0 + i, t0, t0 + P, result[:, i, :])
+                nc.sync.dma_start(out=out_tiles[:, m0 : m0 + 2, t0 : t0 + P], in_=result[:])

@@ -18,6 +18,7 @@ P = 128
 PACK = 4
 HALF = S // 2
 M_TILES = S // P
+LINE = 4
 PREFIX = N - HALF
 
 
@@ -67,7 +68,10 @@ def tile_picked_neuron_lin_gelu_srt_e_kernel(tc, w, xT, b, offs, out):
 
         x_bf = keep.tile([P, T, PACK], BF16, name="x_bf", align_bytes=64)
         for h in range(2):
-            nc.scalar.copy(out=x_bf[:, h * P : (h + 1) * P, :], in_=x_raw[h][:].rearrange("p j t -> p t j"))
+            nc.scalar.copy(
+                out=x_bf[:, h * P : (h + 1) * P, :].rearrange("p (c i) j -> p c j i", i=LINE),
+                in_=x_raw[h][:].rearrange("p j (c i) -> p c j i", i=LINE),
+            )
 
         codes = keep.tile([P, S], U32, name="w_codes", tag="x_raw0", align_bytes=64)
         w_codes = [codes[:, m * P : (m + 1) * P] for m in range(M_TILES)]

@@ -38,10 +38,9 @@ def tile_picked_neuron_lin_gelu_srt_e_kernel(tc, w, xT, b, offs, out):
             nc.sync.dma_start(out=planes[j][:], in_=w_rows[:, j, :])
         last = planes[PACK - 1]
         nc.sync.dma_start(out=last[:, :PREFIX], in_=w_rows[:, PACK - 1, :PREFIX])
+        nc.sync.dma_start(out=last[:, PREFIX:], in_=w_rows[:, PACK - 1, PREFIX:])
         x_raw = []
         for h in range(2):
-            if h == 1:
-                nc.sync.dma_start(out=last[:, PREFIX:], in_=w_rows[:, PACK - 1, PREFIX:])
             raw = keep.tile([P, PACK, P], F32, name=f"x_raw{h}", tag=f"x_raw{h}", align_bytes=64)
             nc.sync.dma_start(out=raw[:], in_=x_rows[:, :, h * P : (h + 1) * P])
             x_raw.append(raw)
@@ -60,11 +59,11 @@ def tile_picked_neuron_lin_gelu_srt_e_kernel(tc, w, xT, b, offs, out):
         bias = keep.tile([P, M_TILES], F32, name="bias")
         nc.scalar.copy(out=bias[:], in_=b_turned[:, 0:M_TILES])
 
-        w_bf = keep.tile([P, S, PACK], BF16, name="w_bf", align_bytes=64)
-        for j in range(PACK - 1):
-            nc.vector.tensor_copy(out=w_bf[:, :, j], in_=planes[j][:].indirect(offsets[:]))
-        nc.vector.tensor_copy(out=w_bf[:, :HALF, PACK - 1], in_=last[:, :PREFIX].indirect(offsets[:, : HALF // 16]))
-        nc.vector.tensor_copy(out=w_bf[:, HALF:, PACK - 1], in_=last[:].indirect(offsets[:, HALF // 16 :]))
+        w_bf = [keep.tile([P, HALF, PACK], BF16, name=f"w_bf{h}", align_bytes=64) for h in range(2)]
+        for j in range(PACK):
+            window = planes[j][:, :PREFIX]
+            nc.vector.tensor_copy(out=w_bf[0][:, :, j], in_=window.indirect(offsets[:, : HALF // 16]))
+            nc.vector.tensor_copy(out=w_bf[1][:, :, j], in_=planes[j][:].indirect(offsets[:, HALF // 16 :]))
 
         x_bf = keep.tile([P, T, PACK], BF16, name="x_bf", align_bytes=64)
         for h in range(2):
@@ -79,19 +78,16 @@ def tile_picked_neuron_lin_gelu_srt_e_kernel(tc, w, xT, b, offs, out):
         x_codes = keep.tile([P, T], U32, name="x_codes", align_bytes=64)
         x_scales = keep.tile([P, T], U8, name="x_scales", align_bytes=64)
 
-        def quantise(codes, scales, values, i):
-            cols = slice(i * P, (i + 1) * P)
-            nc.vector.quantize_mx(
-                out=codes.bitcast(FP8X4),
-                scales=scales[:, cols],
-                in_=values[:, cols, :].rearrange("p c j -> p (c j)"),
-            )
+        def quantise(codes, scales, values):
+            nc.vector.quantize_mx(out=codes.bitcast(FP8X4), scales=scales, in_=values.rearrange("p c j -> p (c j)"))
 
         def quantise_w(m):
-            quantise(w_codes[m], w_scales, w_bf, m)
+            i = m % 2
+            quantise(w_codes[m], w_scales[:, m * P : (m + 1) * P], w_bf[m // 2][:, i * P : (i + 1) * P, :])
 
         def quantise_x(h):
-            quantise(x_codes[:, h * P : (h + 1) * P], x_scales, x_bf, h)
+            tokens = slice(h * P, (h + 1) * P)
+            quantise(x_codes[:, tokens], x_scales[:, tokens], x_bf[:, tokens, :])
 
         quantise_w(0)
         quantise_x(0)

@@ -39,11 +39,8 @@ def tile_picked_neuron_lin_gelu_srt_e_kernel(tc, w, xT, b, offs, out):
         last = planes[PACK - 1]
         nc.sync.dma_start(out=last[:, :PREFIX], in_=w_rows[:, PACK - 1, :PREFIX])
         nc.sync.dma_start(out=last[:, PREFIX:], in_=w_rows[:, PACK - 1, PREFIX:])
-        x_raw = []
-        for h in range(2):
-            raw = keep.tile([P, PACK, P], F32, name=f"x_raw{h}", tag=f"x_raw{h}", align_bytes=64)
-            nc.sync.dma_start(out=raw[:], in_=x_rows[:, :, h * P : (h + 1) * P])
-            x_raw.append(raw)
+        x_raw = keep.tile([P, PACK, T], F32, name="x_raw", align_bytes=64)
+        nc.sync.dma_start(out=x_raw[:], in_=x_rows)
 
         b_rows = keep.tile([P, P], F32, name="b_rows", align_bytes=64)
         nc.vector.memset(b_rows[:], 0.0)
@@ -54,50 +51,65 @@ def tile_picked_neuron_lin_gelu_srt_e_kernel(tc, w, xT, b, offs, out):
         make_identity(nc, ident[:])
         table = keep.tile([P, 1], F32, name="table")
         nc.scalar.activation(out=table[:], in_=warm[:], func=ACT.Gelu_apprx_tanh)
-        b_turned = psum.tile([P, P], F32, name="b_turned", tag="bank3_128")
+        b_turned = psum.tile([P, P], F32, name="b_turned", tag="bank3_0")
         nc.tensor.transpose(b_turned[:], b_rows[:], ident[:])
         bias = keep.tile([P, M_TILES], F32, name="bias")
         nc.scalar.copy(out=bias[:], in_=b_turned[:, 0:M_TILES])
 
-        w_bf = [keep.tile([P, HALF, PACK], BF16, name=f"w_bf{h}", align_bytes=64) for h in range(2)]
+        pairs = keep.tile([P, 2, HALF, 2], BF16, name="pairs", align_bytes=64)
+        w_high = keep.tile([P, HALF, PACK], BF16, name="w_high", align_bytes=64)
         for j in range(PACK):
             window = planes[j][:, :PREFIX]
-            nc.vector.tensor_copy(out=w_bf[0][:, :, j], in_=window.indirect(offsets[:, : HALF // 16]))
-            nc.vector.tensor_copy(out=w_bf[1][:, :, j], in_=planes[j][:].indirect(offsets[:, HALF // 16 :]))
+            nc.vector.tensor_copy(out=pairs[:, j // 2, :, j % 2], in_=window.indirect(offsets[:, : HALF // 16]))
+            nc.vector.tensor_copy(out=w_high[:, :, j], in_=planes[j][:].indirect(offsets[:, HALF // 16 :]))
 
-        x_bf = keep.tile([P, T, PACK], BF16, name="x_bf", align_bytes=64)
-        for h in range(2):
+        pair_words = pairs[:].rearrange("p u c e -> p (u c e)").bitcast(U32).rearrange("p (u c) -> p c u", u=2)
+        w_bf = []
+        for m in range(2):
+            woven = keep.tile([P, P * PACK], BF16, name=f"w_low{m}", align_bytes=64)
             nc.scalar.copy(
-                out=x_bf[:, h * P : (h + 1) * P, :].rearrange("p (c i) j -> p c j i", i=LINE),
-                in_=x_raw[h][:].rearrange("p j (c i) -> p c j i", i=LINE),
+                out=woven[:].bitcast(U32).rearrange("p (c u) -> p c u", u=2),
+                in_=pair_words[:, m * P : (m + 1) * P, :],
             )
+            w_bf.append(woven[:])
+        for i in range(2):
+            w_bf.append(w_high[:, i * P : (i + 1) * P, :].rearrange("p c j -> p (c j)"))
 
-        codes = keep.tile([P, S], U32, name="w_codes", tag="x_raw0", align_bytes=64)
-        w_codes = [codes[:, m * P : (m + 1) * P] for m in range(M_TILES)]
+        first_codes = keep.tile([P, P], U32, name="first_codes", align_bytes=64)
         w_scales = keep.tile([P, S], U8, name="w_scales", align_bytes=64)
         x_codes = keep.tile([P, T], U32, name="x_codes", align_bytes=64)
         x_scales = keep.tile([P, T], U8, name="x_scales", align_bytes=64)
+        x_bf = [keep.tile([P, P, PACK], BF16, name=f"x_bf{h}", tag=f"x_bf{h}", align_bytes=64) for h in range(2)]
 
-        def quantise(codes, scales, values):
-            nc.vector.quantize_mx(out=codes.bitcast(FP8X4), scales=scales, in_=values.rearrange("p c j -> p (c j)"))
+        def interleave_x(copy, h):
+            copy(
+                out=x_bf[h][:].rearrange("p (c i) j -> p c j i", i=LINE),
+                in_=x_raw[:, :, h * P : (h + 1) * P].rearrange("p j (c i) -> p c j i", i=LINE),
+            )
 
         def quantise_w(m):
-            i = m % 2
-            quantise(w_codes[m], w_scales[:, m * P : (m + 1) * P], w_bf[m // 2][:, i * P : (i + 1) * P, :])
+            nc.vector.quantize_mx(out=w_codes[m].bitcast(FP8X4), scales=w_scales[:, m * P : (m + 1) * P], in_=w_bf[m])
 
         def quantise_x(h):
             tokens = slice(h * P, (h + 1) * P)
-            quantise(x_codes[:, tokens], x_scales[:, tokens], x_bf[:, tokens, :])
+            values = x_bf[h][:].rearrange("p c j -> p (c j)")
+            nc.vector.quantize_mx(out=x_codes[:, tokens].bitcast(FP8X4), scales=x_scales[:, tokens], in_=values)
 
+        w_codes = [first_codes[:]]
         quantise_w(0)
+        interleave_x(nc.vector.tensor_copy, 0)
+        interleave_x(nc.scalar.copy, 1)
         quantise_x(0)
+        quantise_x(1)
+        later_codes = keep.tile([P, S - P], U32, name="later_codes", tag="x_bf0", align_bytes=64)
+        w_codes.extend([later_codes[:, i * P : (i + 1) * P] for i in range(M_TILES - 1)])
         for m in range(1, M_TILES):
             quantise_w(m)
-        quantise_x(1)
 
         out_tiles = out.rearrange("(m p) t -> p m t", p=P)
+        results = [keep.tile([P, T], F32, name=f"result{m}", align_bytes=64) for m in range(M_TILES)]
 
-        def product(m, t0, t1, result):
+        def product(m, t0, t1):
             tokens = slice(t0, t1)
             cols = slice(m * P, (m + 1) * P)
             acc = psum.tile([P, t1 - t0], F32, name=f"acc{m}_{t0}", tag=f"bank{m}_{t0}")
@@ -111,12 +123,12 @@ def tile_picked_neuron_lin_gelu_srt_e_kernel(tc, w, xT, b, offs, out):
                 stop=True,
             )
             nc.scalar.activation(
-                out=result, in_=acc[:], func=ACT.Gelu_apprx_tanh, bias=bias[:, m : m + 1]
+                out=results[m][:, tokens], in_=acc[:], func=ACT.Gelu_apprx_tanh, bias=bias[:, m : m + 1]
             )
+            if t1 == T:
+                nc.sync.dma_start(out=out_tiles[:, m, :], in_=results[m][:])
 
         for t0 in range(0, T, P):
-            for m0 in range(0, M_TILES, 2):
-                result = keep.tile([P, 2, P], F32, name=f"result{m0}_{t0}", align_bytes=64)
-                for i in range(2):
-                    product(m0 + i, t0, t0 + P, result[:, i, :])
-                nc.sync.dma_start(out=out_tiles[:, m0 : m0 + 2, t0 : t0 + P], in_=result[:])
+            product(0, t0, t0 + P)
+        for m in range(1, M_TILES):
+            product(m, 0, T)

@@ -46,7 +46,7 @@ def tile_picked_neuron_lin_gelu_srt_e_kernel(tc, w, xT, b, offs, out):
         nc.vector.memset(b_rows[:], 0.0)
         warm = keep.tile([P, 1], F32, name="warm")
         nc.vector.memset(warm[:], 0.0)
-        nc.scalar.dma_start(out=b_rows[0:M_TILES, :], in_=b.rearrange("(m p) o -> m (p o)", p=P))
+        nc.sync.dma_start(out=b_rows[0:M_TILES, :], in_=b.rearrange("(m p) o -> m (p o)", p=P))
         ident = keep.tile([P, P], F32, name="ident", align_bytes=64)
         make_identity(nc, ident[:])
         table = keep.tile([P, 1], F32, name="table")
@@ -125,8 +125,7 @@ def tile_picked_neuron_lin_gelu_srt_e_kernel(tc, w, xT, b, offs, out):
             nc.scalar.activation(
                 out=results[m][:, tokens], in_=acc[:], func=ACT.Gelu_apprx_tanh, bias=bias[:, m : m + 1]
             )
-            if t1 == T:
-                nc.sync.dma_start(out=out_tiles[:, m, :], in_=results[m][:])
+            nc.sync.dma_start(out=out_tiles[:, m, tokens], in_=results[m][:, tokens])
 
         for t0 in range(0, T, P):
             product(0, t0, t0 + P)

@@ -19,6 +19,7 @@ PACK = 4
 HALF = S // 2
 M_TILES = S // P
 LINE = 4
+SHARE = 64
 PREFIX = N - HALF
 
 
@@ -32,102 +33,99 @@ def tile_picked_neuron_lin_gelu_srt_e_kernel(tc, w, xT, b, offs, out):
         x_rows = xT.rearrange("(p j) t -> p j t", j=PACK)
         planes = [keep.tile([P, N], F32, name=f"plane{j}", align_bytes=64) for j in range(PACK)]
         offsets = keep.tile([P, S // 16], U16, name="offsets")
+        b_rows = keep.tile([P, P], F32, name="b_rows", align_bytes=64)
+        nc.vector.memset(b_rows[:], 0.0)
+        warm = keep.tile([P, 1], F32, name="warm")
+        nc.vector.memset(warm[:], 0.0)
         nc.sync.dma_start(out=planes[0][:], in_=w_rows[:, 0, :])
         nc.sync.dma_start(offsets[:], offs)
+        nc.sync.dma_start(out=b_rows[0:M_TILES, :], in_=b.rearrange("(m p) o -> m (p o)", p=P))
         for j in range(1, PACK - 1):
             nc.sync.dma_start(out=planes[j][:], in_=w_rows[:, j, :])
         last = planes[PACK - 1]
         nc.sync.dma_start(out=last[:, :PREFIX], in_=w_rows[:, PACK - 1, :PREFIX])
         nc.sync.dma_start(out=last[:, PREFIX:], in_=w_rows[:, PACK - 1, PREFIX:])
-        x_raw = keep.tile([P, PACK, T], F32, name="x_raw", align_bytes=64)
-        nc.sync.dma_start(out=x_raw[:], in_=x_rows)
+        x_raw = [keep.tile([P, PACK, P], F32, name=f"x_raw{h}", tag=f"x_raw{h}", align_bytes=64) for h in range(2)]
+        for h in range(2):
+            nc.sync.dma_start(out=x_raw[h][:], in_=x_rows[:, :, h * P : (h + 1) * P])
 
-        b_rows = keep.tile([P, P], F32, name="b_rows", align_bytes=64)
-        nc.vector.memset(b_rows[:], 0.0)
-        warm = keep.tile([P, 1], F32, name="warm")
-        nc.vector.memset(warm[:], 0.0)
-        nc.sync.dma_start(out=b_rows[0:M_TILES, :], in_=b.rearrange("(m p) o -> m (p o)", p=P))
         ident = keep.tile([P, P], F32, name="ident", align_bytes=64)
         make_identity(nc, ident[:])
         table = keep.tile([P, 1], F32, name="table")
         nc.scalar.activation(out=table[:], in_=warm[:], func=ACT.Gelu_apprx_tanh)
-        b_turned = psum.tile([P, P], F32, name="b_turned", tag="bank3_0")
+        b_turned = psum.tile([P, P], F32, name="b_turned", tag="bank3_1")
         nc.tensor.transpose(b_turned[:], b_rows[:], ident[:])
         bias = keep.tile([P, M_TILES], F32, name="bias")
         nc.scalar.copy(out=bias[:], in_=b_turned[:, 0:M_TILES])
 
-        pairs = keep.tile([P, 2, HALF, 2], BF16, name="pairs", align_bytes=64)
-        w_high = keep.tile([P, HALF, PACK], BF16, name="w_high", align_bytes=64)
+        pairs = [keep.tile([P, 2, HALF, 2], BF16, name=f"pairs{i}", align_bytes=64) for i in range(2)]
         for j in range(PACK):
-            window = planes[j][:, :PREFIX]
-            nc.vector.tensor_copy(out=pairs[:, j // 2, :, j % 2], in_=window.indirect(offsets[:, : HALF // 16]))
-            nc.vector.tensor_copy(out=w_high[:, :, j], in_=planes[j][:].indirect(offsets[:, HALF // 16 :]))
+            windows = (planes[j][:, :PREFIX], planes[j][:])
+            for i in range(2):
+                entries = offsets[:, i * HALF // 16 : (i + 1) * HALF // 16]
+                nc.vector.tensor_copy(out=pairs[i][:, j // 2, :, j % 2], in_=windows[i].indirect(entries))
 
-        pair_words = pairs[:].rearrange("p u c e -> p (u c e)").bitcast(U32).rearrange("p (u c) -> p c u", u=2)
         w_bf = []
-        for m in range(2):
-            woven = keep.tile([P, P * PACK], BF16, name=f"w_low{m}", align_bytes=64)
+        for m in range(M_TILES):
+            words = pairs[m // 2][:].rearrange("p u c e -> p (u c e)").bitcast(U32).rearrange("p (u c) -> p c u", u=2)
+            woven = keep.tile([P, P * PACK], BF16, name=f"w_bf{m}", align_bytes=64)
             nc.scalar.copy(
                 out=woven[:].bitcast(U32).rearrange("p (c u) -> p c u", u=2),
-                in_=pair_words[:, m * P : (m + 1) * P, :],
+                in_=words[:, (m % 2) * P : (m % 2 + 1) * P, :],
             )
             w_bf.append(woven[:])
-        for i in range(2):
-            w_bf.append(w_high[:, i * P : (i + 1) * P, :].rearrange("p c j -> p (c j)"))
 
-        first_codes = keep.tile([P, P], U32, name="first_codes", align_bytes=64)
         w_scales = keep.tile([P, S], U8, name="w_scales", align_bytes=64)
         x_codes = keep.tile([P, T], U32, name="x_codes", align_bytes=64)
         x_scales = keep.tile([P, T], U8, name="x_scales", align_bytes=64)
-        x_bf = [keep.tile([P, P, PACK], BF16, name=f"x_bf{h}", tag=f"x_bf{h}", align_bytes=64) for h in range(2)]
 
-        def interleave_x(copy, h):
+        def interleave_x(copy, rounded, h, t0, t1):
             copy(
-                out=x_bf[h][:].rearrange("p (c i) j -> p c j i", i=LINE),
-                in_=x_raw[:, :, h * P : (h + 1) * P].rearrange("p j (c i) -> p c j i", i=LINE),
+                out=rounded[:].rearrange("p (c i) j -> p c j i", i=LINE),
+                in_=x_raw[h][:, :, t0:t1].rearrange("p j (c i) -> p c j i", i=LINE),
             )
 
         def quantise_w(m):
-            nc.vector.quantize_mx(out=w_codes[m].bitcast(FP8X4), scales=w_scales[:, m * P : (m + 1) * P], in_=w_bf[m])
+            cols = slice(m * P, (m + 1) * P)
+            nc.vector.quantize_mx(out=w_codes[:, cols].bitcast(FP8X4), scales=w_scales[:, cols], in_=w_bf[m])
 
-        def quantise_x(h):
-            tokens = slice(h * P, (h + 1) * P)
-            values = x_bf[h][:].rearrange("p c j -> p (c j)")
-            nc.vector.quantize_mx(out=x_codes[:, tokens].bitcast(FP8X4), scales=x_scales[:, tokens], in_=values)
+        def quantise_x(rounded, t0, t1):
+            values = rounded[:].rearrange("p c j -> p (c j)")
+            nc.vector.quantize_mx(out=x_codes[:, t0:t1].bitcast(FP8X4), scales=x_scales[:, t0:t1], in_=values)
 
-        w_codes = [first_codes[:]]
+        x_first = keep.tile([P, P, PACK], BF16, name="x_first", tag="x_first", align_bytes=64)
+        interleave_x(nc.vector.tensor_copy, x_first, 0, 0, P)
+        quantise_x(x_first, 0, P)
+        w_codes = keep.tile([P, S], U32, name="w_codes", tag="x_raw0", align_bytes=64)
         quantise_w(0)
-        interleave_x(nc.vector.tensor_copy, 0)
-        interleave_x(nc.scalar.copy, 1)
-        quantise_x(0)
-        quantise_x(1)
-        later_codes = keep.tile([P, S - P], U32, name="later_codes", tag="x_bf0", align_bytes=64)
-        w_codes.extend([later_codes[:, i * P : (i + 1) * P] for i in range(M_TILES - 1)])
-        for m in range(1, M_TILES):
-            quantise_w(m)
+        quantise_w(1)
+        x_share = keep.tile([P, SHARE, PACK], BF16, name="x_share", tag="x_first", align_bytes=64)
+        x_rest = keep.tile([P, P - SHARE, PACK], BF16, name="x_rest", align_bytes=64)
+        interleave_x(nc.vector.tensor_copy, x_share, 1, 0, SHARE)
+        interleave_x(nc.scalar.copy, x_rest, 1, SHARE, P)
+        quantise_w(2)
+        quantise_w(3)
+        quantise_x(x_share, P, P + SHARE)
+        quantise_x(x_rest, P + SHARE, T)
 
         out_tiles = out.rearrange("(m p) t -> p m t", p=P)
-        results = [keep.tile([P, T], F32, name=f"result{m}", align_bytes=64) for m in range(M_TILES)]
-
-        def product(m, t0, t1):
-            tokens = slice(t0, t1)
-            cols = slice(m * P, (m + 1) * P)
-            acc = psum.tile([P, t1 - t0], F32, name=f"acc{m}_{t0}", tag=f"bank{m}_{t0}")
-            nc.tensor.matmul_mx(
-                out=acc[:],
-                lhsT=w_codes[m].bitcast(FP8X4),
-                lhsT_scale=w_scales[:, cols],
-                rhs=x_codes[:, tokens].bitcast(FP8X4),
-                rhs_scale=x_scales[:, tokens],
-                start=True,
-                stop=True,
-            )
-            nc.scalar.activation(
-                out=results[m][:, tokens], in_=acc[:], func=ACT.Gelu_apprx_tanh, bias=bias[:, m : m + 1]
-            )
-            nc.sync.dma_start(out=out_tiles[:, m, tokens], in_=results[m][:, tokens])
-
-        for t0 in range(0, T, P):
-            product(0, t0, t0 + P)
-        for m in range(1, M_TILES):
-            product(m, 0, T)
+        for h in range(2):
+            tokens = slice(h * P, (h + 1) * P)
+            for i in range(2):
+                result = keep.tile([P, 2, P], F32, name=f"result{h}_{i}", align_bytes=64)
+                for m in range(2 * i, 2 * i + 2):
+                    cols = slice(m * P, (m + 1) * P)
+                    acc = psum.tile([P, P], F32, name=f"acc{m}_{h}", tag=f"bank{m}_{h}")
+                    nc.tensor.matmul_mx(
+                        out=acc[:],
+                        lhsT=w_codes[:, cols].bitcast(FP8X4),
+                        lhsT_scale=w_scales[:, cols],
+                        rhs=x_codes[:, tokens].bitcast(FP8X4),
+                        rhs_scale=x_scales[:, tokens],
+                        start=True,
+                        stop=True,
+                    )
+                    nc.scalar.activation(
+                        out=result[:, m % 2, :], in_=acc[:], func=ACT.Gelu_apprx_tanh, bias=bias[:, m : m + 1]
+                    )
+                nc.sync.dma_start(out=out_tiles[:, 2 * i : 2 * i + 2, tokens], in_=result[:])

@@ -93,13 +93,15 @@ def tile_picked_neuron_lin_gelu_srt_e_kernel(tc, w, xT, b, offs, out):
             values = rounded[:].rearrange("p c j -> p (c j)")
             nc.vector.quantize_mx(out=x_codes[:, t0:t1].bitcast(FP8X4), scales=x_scales[:, t0:t1], in_=values)
 
-        x_first = keep.tile([P, P, PACK], BF16, name="x_first", tag="x_first", align_bytes=64)
-        interleave_x(nc.vector.tensor_copy, x_first, 0, 0, P)
-        quantise_x(x_first, 0, P)
+        x_first = [keep.tile([P, SHARE, PACK], BF16, name=f"x_first{i}", tag=f"x_first{i}", align_bytes=64) for i in range(2)]
+        for i in range(2):
+            interleave_x(nc.vector.tensor_copy, x_first[i], 0, i * SHARE, (i + 1) * SHARE)
+        for i in range(2):
+            quantise_x(x_first[i], i * SHARE, (i + 1) * SHARE)
         w_codes = keep.tile([P, S], U32, name="w_codes", tag="x_raw0", align_bytes=64)
         quantise_w(0)
         quantise_w(1)
-        x_share = keep.tile([P, SHARE, PACK], BF16, name="x_share", tag="x_first", align_bytes=64)
+        x_share = keep.tile([P, SHARE, PACK], BF16, name="x_share", tag="x_first1", align_bytes=64)
         x_rest = keep.tile([P, P - SHARE, PACK], BF16, name="x_rest", align_bytes=64)
         interleave_x(nc.vector.tensor_copy, x_share, 1, 0, SHARE)
         interleave_x(nc.scalar.copy, x_rest, 1, SHARE, P)

@@ -20,6 +20,7 @@ HALF = S // 2
 M_TILES = S // P
 LINE = 4
 SHARE = 64
+STORES = ((1, 1, 1, 1), (2, 2))
 PREFIX = N - HALF
 
 
@@ -39,7 +40,9 @@ def tile_picked_neuron_lin_gelu_srt_e_kernel(tc, w, xT, b, offs, out):
         nc.vector.memset(warm[:], 0.0)
         nc.sync.dma_start(out=planes[0][:], in_=w_rows[:, 0, :])
         nc.sync.dma_start(offsets[:], offs)
-        nc.sync.dma_start(out=b_rows[0:M_TILES, :], in_=b.rearrange("(m p) o -> m (p o)", p=P))
+        b_tiles = b.rearrange("(m p) o -> m (p o)", p=P)
+        for i in range(2):
+            nc.sync.dma_start(out=b_rows[2 * i : 2 * i + 2, :], in_=b_tiles[2 * i : 2 * i + 2, :])
         for j in range(1, PACK - 1):
             nc.sync.dma_start(out=planes[j][:], in_=w_rows[:, j, :])
         last = planes[PACK - 1]
@@ -111,11 +114,12 @@ def tile_picked_neuron_lin_gelu_srt_e_kernel(tc, w, xT, b, offs, out):
         quantise_x(x_rest, P + SHARE, T)
 
         out_tiles = out.rearrange("(m p) t -> p m t", p=P)
-        for h in range(2):
+        for h, groups in enumerate(STORES):
             tokens = slice(h * P, (h + 1) * P)
-            for i in range(2):
-                result = keep.tile([P, 2, P], F32, name=f"result{h}_{i}", align_bytes=64)
-                for m in range(2 * i, 2 * i + 2):
+            first = 0
+            for group in groups:
+                result = keep.tile([P, group, P], F32, name=f"result{h}_{first}", align_bytes=64)
+                for m in range(first, first + group):
                     cols = slice(m * P, (m + 1) * P)
                     acc = psum.tile([P, P], F32, name=f"acc{m}_{h}", tag=f"bank{m}_{h}")
                     nc.tensor.matmul_mx(
@@ -128,6 +132,7 @@ def tile_picked_neuron_lin_gelu_srt_e_kernel(tc, w, xT, b, offs, out):
                         stop=True,
                     )
                     nc.scalar.activation(
-                        out=result[:, m % 2, :], in_=acc[:], func=ACT.Gelu_apprx_tanh, bias=bias[:, m : m + 1]
+                        out=result[:, m - first, :], in_=acc[:], func=ACT.Gelu_apprx_tanh, bias=bias[:, m : m + 1]
                     )
-                nc.sync.dma_start(out=out_tiles[:, 2 * i : 2 * i + 2, tokens], in_=result[:])
+                nc.sync.dma_start(out=out_tiles[:, first : first + group, tokens], in_=result[:])
+                first = first + group

@@ -18,6 +18,7 @@ P = 128
 PACK = 4
 HALF = S // 2
 M_TILES = S // P
+BURST = 256
 LINE = 4
 SHARE = 64
 STORES = ((1, 1, 1, 1), (2, 2))
@@ -32,7 +33,7 @@ def tile_picked_neuron_lin_gelu_srt_e_kernel(tc, w, xT, b, offs, out):
 
         w_rows = w.rearrange("(p j) n -> p j n", j=PACK)
         x_rows = xT.rearrange("(p j) t -> p j t", j=PACK)
-        planes = [keep.tile([P, N], F32, name=f"plane{j}", align_bytes=64) for j in range(PACK)]
+        planes = [keep.tile([P, N], F32, name=f"plane{j}", align_bytes=BURST) for j in range(PACK)]
         offsets = keep.tile([P, S // 16], U16, name="offsets")
         b_rows = keep.tile([P, P], F32, name="b_rows", align_bytes=64)
         nc.vector.memset(b_rows[:], 0.0)
@@ -48,7 +49,7 @@ def tile_picked_neuron_lin_gelu_srt_e_kernel(tc, w, xT, b, offs, out):
         last = planes[PACK - 1]
         nc.sync.dma_start(out=last[:, :PREFIX], in_=w_rows[:, PACK - 1, :PREFIX])
         nc.sync.dma_start(out=last[:, PREFIX:], in_=w_rows[:, PACK - 1, PREFIX:])
-        x_raw = [keep.tile([P, PACK, P], F32, name=f"x_raw{h}", tag=f"x_raw{h}", align_bytes=64) for h in range(2)]
+        x_raw = [keep.tile([P, PACK, P], F32, name=f"x_raw{h}", tag=f"x_raw{h}", align_bytes=BURST) for h in range(2)]
         for h in range(2):
             nc.sync.dma_start(out=x_raw[h][:], in_=x_rows[:, :, h * P : (h + 1) * P])
 
@@ -101,7 +102,7 @@ def tile_picked_neuron_lin_gelu_srt_e_kernel(tc, w, xT, b, offs, out):
             interleave_x(nc.vector.tensor_copy, x_first[i], 0, i * SHARE, (i + 1) * SHARE)
         for i in range(2):
             quantise_x(x_first[i], i * SHARE, (i + 1) * SHARE)
-        w_codes = keep.tile([P, S], U32, name="w_codes", tag="x_raw0", align_bytes=64)
+        w_codes = keep.tile([P, S], U32, name="w_codes", tag="x_raw0", align_bytes=BURST)
         quantise_w(0)
         quantise_w(1)
         x_share = keep.tile([P, SHARE, PACK], BF16, name="x_share", tag="x_first1", align_bytes=64)
@@ -118,7 +119,7 @@ def tile_picked_neuron_lin_gelu_srt_e_kernel(tc, w, xT, b, offs, out):
             tokens = slice(h * P, (h + 1) * P)
             first = 0
             for group in groups:
-                result = keep.tile([P, group, P], F32, name=f"result{h}_{first}", align_bytes=64)
+                result = keep.tile([P, group, P], F32, name=f"result{h}_{first}", align_bytes=BURST)
                 for m in range(first, first + group):
                     cols = slice(m * P, (m + 1) * P)
                     acc = psum.tile([P, P], F32, name=f"acc{m}_{h}", tag=f"bank{m}_{h}")

@@ -43,7 +43,7 @@ def tile_picked_neuron_lin_gelu_srt_e_kernel(tc, w, xT, b, offs, out):
         nc.sync.dma_start(offsets[:], offs)
         b_tiles = b.rearrange("(m p) o -> m (p o)", p=P)
         for i in range(2):
-            nc.sync.dma_start(out=b_rows[2 * i : 2 * i + 2, :], in_=b_tiles[2 * i : 2 * i + 2, :])
+            nc.scalar.dma_start(out=b_rows[2 * i : 2 * i + 2, :], in_=b_tiles[2 * i : 2 * i + 2, :])
         for j in range(1, PACK - 1):
             nc.sync.dma_start(out=planes[j][:], in_=w_rows[:, j, :])
         last = planes[PACK - 1]

from contextlib import ExitStack

import concourse.mybir as mybir
from concourse.masks import make_identity

K, N, S, T = 512, 2048, 512, 256
FLOPS = 2 * K * S * T

F32 = mybir.dt.float32
BF16 = mybir.dt.bfloat16
U32 = mybir.dt.uint32
U16 = mybir.dt.uint16
U8 = mybir.dt.uint8
FP8X4 = mybir.dt.float8_e4m3fn_x4
ACT = mybir.ActivationFunctionType

P = 128
PACK = 4
HALF = S // 2
M_TILES = S // P
BURST = 256
LINE = 4
SHARE = 64
STORES = ((1, 1, 1, 1), (2, 2))
PREFIX = N - HALF


def tile_picked_neuron_lin_gelu_srt_e_kernel(tc, w, xT, b, offs, out):
    nc = tc.nc
    with ExitStack() as ctx:
        keep = ctx.enter_context(tc.tile_pool(name="keep", bufs=1))
        psum = ctx.enter_context(tc.psum_pool(name="psum", bufs=1))

        w_rows = w.rearrange("(p j) n -> p j n", j=PACK)
        x_rows = xT.rearrange("(p j) t -> p j t", j=PACK)
        planes = [keep.tile([P, N], F32, name=f"plane{j}", align_bytes=BURST) for j in range(PACK)]
        offsets = keep.tile([P, S // 16], U16, name="offsets")
        b_rows = keep.tile([P, P], F32, name="b_rows", align_bytes=64)
        nc.vector.memset(b_rows[:], 0.0)
        warm = keep.tile([P, 1], F32, name="warm")
        nc.vector.memset(warm[:], 0.0)
        nc.sync.dma_start(out=planes[0][:], in_=w_rows[:, 0, :])
        nc.sync.dma_start(offsets[:], offs)
        b_tiles = b.rearrange("(m p) o -> m (p o)", p=P)
        for i in range(2):
            nc.scalar.dma_start(out=b_rows[2 * i : 2 * i + 2, :], in_=b_tiles[2 * i : 2 * i + 2, :])
        for j in range(1, PACK - 1):
            nc.sync.dma_start(out=planes[j][:], in_=w_rows[:, j, :])
        last = planes[PACK - 1]
        nc.sync.dma_start(out=last[:, :PREFIX], in_=w_rows[:, PACK - 1, :PREFIX])
        nc.sync.dma_start(out=last[:, PREFIX:], in_=w_rows[:, PACK - 1, PREFIX:])
        x_raw = [keep.tile([P, PACK, P], F32, name=f"x_raw{h}", tag=f"x_raw{h}", align_bytes=BURST) for h in range(2)]
        for h in range(2):
            nc.sync.dma_start(out=x_raw[h][:], in_=x_rows[:, :, h * P : (h + 1) * P])

        ident = keep.tile([P, P], F32, name="ident", align_bytes=64)
        make_identity(nc, ident[:])
        table = keep.tile([P, 1], F32, name="table")
        nc.scalar.activation(out=table[:], in_=warm[:], func=ACT.Gelu_apprx_tanh)
        b_turned = psum.tile([P, P], F32, name="b_turned", tag="bank3_1")
        nc.tensor.transpose(b_turned[:], b_rows[:], ident[:])
        bias = keep.tile([P, M_TILES], F32, name="bias")
        nc.scalar.copy(out=bias[:], in_=b_turned[:, 0:M_TILES])

        pairs = [keep.tile([P, 2, HALF, 2], BF16, name=f"pairs{i}", align_bytes=64) for i in range(2)]
        for j in range(PACK):
            windows = (planes[j][:, :PREFIX], planes[j][:])
            for i in range(2):
                entries = offsets[:, i * HALF // 16 : (i + 1) * HALF // 16]
                nc.vector.tensor_copy(out=pairs[i][:, j // 2, :, j % 2], in_=windows[i].indirect(entries))

        w_bf = []
        for m in range(M_TILES):
            words = pairs[m // 2][:].rearrange("p u c e -> p (u c e)").bitcast(U32).rearrange("p (u c) -> p c u", u=2)
            woven = keep.tile([P, P * PACK], BF16, name=f"w_bf{m}", align_bytes=64)
            nc.scalar.copy(
                out=woven[:].bitcast(U32).rearrange("p (c u) -> p c u", u=2),
                in_=words[:, (m % 2) * P : (m % 2 + 1) * P, :],
            )
            w_bf.append(woven[:])

        w_scales = keep.tile([P, S], U8, name="w_scales", align_bytes=64)
        x_codes = keep.tile([P, T], U32, name="x_codes", align_bytes=64)
        x_scales = keep.tile([P, T], U8, name="x_scales", align_bytes=64)

        def interleave_x(copy, rounded, h, t0, t1):
            copy(
                out=rounded[:].rearrange("p (c i) j -> p c j i", i=LINE),
                in_=x_raw[h][:, :, t0:t1].rearrange("p j (c i) -> p c j i", i=LINE),
            )

        def quantise_w(m):
            cols = slice(m * P, (m + 1) * P)
            nc.vector.quantize_mx(out=w_codes[:, cols].bitcast(FP8X4), scales=w_scales[:, cols], in_=w_bf[m])

        def quantise_x(rounded, t0, t1):
            values = rounded[:].rearrange("p c j -> p (c j)")
            nc.vector.quantize_mx(out=x_codes[:, t0:t1].bitcast(FP8X4), scales=x_scales[:, t0:t1], in_=values)

        x_first = [keep.tile([P, SHARE, PACK], BF16, name=f"x_first{i}", tag=f"x_first{i}", align_bytes=64) for i in range(2)]
        for i in range(2):
            interleave_x(nc.vector.tensor_copy, x_first[i], 0, i * SHARE, (i + 1) * SHARE)
        for i in range(2):
            quantise_x(x_first[i], i * SHARE, (i + 1) * SHARE)
        w_codes = keep.tile([P, S], U32, name="w_codes", tag="x_raw0", align_bytes=BURST)
        quantise_w(0)
        quantise_w(1)
        x_share = keep.tile([P, SHARE, PACK], BF16, name="x_share", tag="x_first1", align_bytes=64)
        x_rest = keep.tile([P, P - SHARE, PACK], BF16, name="x_rest", align_bytes=64)
        interleave_x(nc.vector.tensor_copy, x_share, 1, 0, SHARE)
        interleave_x(nc.scalar.copy, x_rest, 1, SHARE, P)
        quantise_w(2)
        quantise_w(3)
        quantise_x(x_share, P, P + SHARE)
        quantise_x(x_rest, P + SHARE, T)

        out_tiles = out.rearrange("(m p) t -> p m t", p=P)
        for h, groups in enumerate(STORES):
            tokens = slice(h * P, (h + 1) * P)
            first = 0
            for group in groups:
                result = keep.tile([P, group, P], F32, name=f"result{h}_{first}", align_bytes=BURST)
                for m in range(first, first + group):
                    cols = slice(m * P, (m + 1) * P)
                    acc = psum.tile([P, P], F32, name=f"acc{m}_{h}", tag=f"bank{m}_{h}")
                    nc.tensor.matmul_mx(
                        out=acc[:],
                        lhsT=w_codes[:, cols].bitcast(FP8X4),
                        lhsT_scale=w_scales[:, cols],
                        rhs=x_codes[:, tokens].bitcast(FP8X4),
                        rhs_scale=x_scales[:, tokens],
                        start=True,
                        stop=True,
                    )
                    nc.scalar.activation(
                        out=result[:, m - first, :], in_=acc[:], func=ACT.Gelu_apprx_tanh, bias=bias[:, m : m + 1]
                    )
                nc.sync.dma_start(out=out_tiles[:, first : first + group, tokens], in_=result[:])
                first = first + group
